import numpy as np
import ml_dtypes


def mxq(x, axis, fmt="e4m3"):
    dtype, down = {"e4m3": (ml_dtypes.float8_e4m3fn, 7), "e5m2": (ml_dtypes.float8_e5m2, 14)}[fmt]
    v = np.moveaxis(np.asarray(x, np.float32).astype(ml_dtypes.bfloat16).astype(np.float64), axis, -1)
    blocks = v.reshape(v.shape[:-1] + (-1, 32))
    amax = np.abs(blocks).max(-1, keepdims=True)
    byte = np.maximum(np.where(amax > 0, np.frexp(amax)[1] - 1 + 127, 0) - down, 1)
    scale = np.exp2(byte - 127.0)
    codes = (blocks / scale).astype(np.float32).astype(dtype).astype(np.float64)
    return np.moveaxis((codes * scale).reshape(v.shape), -1, axis)


WIDE = False


def mx_kscale(k, group=512):
    if not WIDE:
        return np.ones(k)
    levels = np.array([18, -18])
    if group != 512:
        return np.exp2(np.random.permutation(np.resize(levels, k // group))).repeat(group)
    if k % 512:
        return np.exp2(np.random.permutation(np.resize(levels, k // 32))).repeat(32)
    a = np.empty((k // 512, 16))
    for p in range(k // 512):
        a[p, :8] = np.random.permutation(np.resize(levels, 8))
        for g in range(8):
            far = levels[np.abs(levels - a[p, g]) >= 10]
            a[p, g + 8] = far[np.random.randint(len(far))]
    return np.exp2(a.ravel()).repeat(32)


def f64(x):
    return np.asarray(x).astype(np.float64)


def sigmoid(v):
    return 1.0 / (1.0 + np.exp(-v))


def bf(x):
    return np.asarray(x, np.float32).astype(ml_dtypes.bfloat16)


def planes(Y):
    r, m = Y.shape
    b = f64(bf(Y)).reshape(r // 32, 32, m)
    amax = np.abs(b).max(1)
    byte = np.clip(np.where(amax > 0, np.frexp(amax)[1] - 1 + 127 - 7, 1), 1, 254)
    codes = (b * np.exp2(127.0 - byte)[:, None, :]).reshape(r, m).astype(np.float32).astype(ml_dtypes.float8_e4m3fn).view(np.uint8)
    words = codes.reshape(r // 512, 128, 4, m).transpose(0, 1, 3, 2)
    return np.ascontiguousarray(words), np.ascontiguousarray(byte.astype(np.uint8).reshape(r // 512, 16, m))


G, D, I, Q, E = 8, 128, 128, 128, 128


def sgn(shape):
    return np.random.uniform(0.5, 2.0, shape) * np.where(np.random.standard_normal(shape) < 0, -1.0, 1.0)


def setup_inputs():
    n = np.random.standard_normal
    s_d = mx_kscale(D, 0)
    s_i = mx_kscale(I, 0)
    return {
        "kT": (n((G, D, I)) / np.sqrt(D) / s_d[:, None]).astype(np.float32),
        "qT": (n((G, D, Q)) * s_d[:, None]).astype(np.float32),
        "kb": (n((G, I, 1))).astype(np.float32),
        "t": (sgn((G, I, 1)) * s_i[:, None]).astype(np.float32),
        "v": ((n((G, I, E))) / s_i[:, None]).astype(np.float32),
        "og": (n((G, Q, E))).astype(np.float32),
    }


def reference(kT, qT, kb, t, v, og):
    kTq = mxq(f64(kT), 1, "e4m3")
    qTq = mxq(f64(qT), 1, "e4m3")
    z = kTq.transpose(0, 2, 1) @ qTq
    p = sigmoid(z + f64(kb)) * f64(t)
    pq = mxq(p, 1, "e4m3")
    vq = mxq(f64(v), 1, "e4m3")
    y = pq.transpose(0, 2, 1) @ vq
    o = y / 16.0 * sigmoid(f64(og))
    Y = o.reshape(G * Q, E)
    words, scales = planes(Y)
    return Y, words, scales

@@ -1,0 +1,214 @@
+from contextlib import ExitStack
+
+import concourse.mybir as mybir
+
+F32 = mybir.dt.float32
+BF16 = mybir.dt.bfloat16
+I32 = mybir.dt.int32
+U32 = mybir.dt.uint32
+U8 = mybir.dt.uint8
+FP8X4 = mybir.dt.float8_e4m3fn_x4
+ALU = mybir.AluOpType
+ACT = mybir.ActivationFunctionType
+
+P = 128
+W = 128
+R = 32
+PACK = 4
+FLOPS = 2 * 2 * 8 * 128 * 128 * 128
+
+MOV = [0, 640]
+STAT = [128, 384]
+
+
+def quantize(nc, codes, scales, start, words, staged):
+    nc.vector.quantize_mx(
+        out=codes[:, start : start + words].bitcast(FP8X4),
+        scales=scales[:, start : start + words],
+        in_=staged,
+    )
+
+
+def products(nc, banks, codes, scales, order):
+    for pair in range(2):
+        for i in range(2):
+            place = 2 * pair + i
+            for slot in range(2):
+                for r in order:
+                    rows = slice(R * r, R * (r + 1))
+                    half = r // 2
+                    c0 = STAT[slot] + 64 * place - 64 * half
+                    m0 = MOV[slot]
+                    nc.tensor.matmul_mx(
+                        out=banks[r][pair][:, i * W : (i + 1) * W],
+                        lhsT=codes[rows, c0 : c0 + W].bitcast(FP8X4),
+                        lhsT_scale=scales[rows, c0 : c0 + W],
+                        rhs=codes[rows, m0 : m0 + W].bitcast(FP8X4),
+                        rhs_scale=scales[rows, m0 : m0 + W],
+                        start=(slot == 0),
+                        stop=(slot == 1),
+                    )
+
+
+def tile_rows_pl_win_sig_gate_kernel(tc, kT, qT, kb, t, v, og, out_0, out_1, out_2):
+    nc = tc.nc
+    with ExitStack() as ctx:
+        sb = ctx.enter_context(tc.tile_pool(name="sb", bufs=1))
+        ps = ctx.enter_context(tc.psum_pool(name="ps", bufs=1))
+        ctx.enter_context(tc.manual_schedule())
+
+        banks = [[ps.tile([P, 512], F32, name="bank%d_%d" % (r, b)) for b in range(2)] for r in range(4)]
+        k_raw = [sb.tile([P, PACK, W], F32, name="k_raw%d" % s) for s in range(2)]
+        q_raw = [sb.tile([P, PACK, W], F32, name="q_raw%d" % s) for s in range(2)]
+        g_raw = [sb.tile([P, PACK * W], F32, name="g_raw%d" % s) for s in range(2)]
+        gate = [sb.tile([P, PACK * W], F32, name="gate%d" % s) for s in range(2)]
+        v_raw = sb.tile([P, 2, PACK, W], F32, name="v_raw")
+        rows_raw = sb.tile([P, 256], F32, name="rows_raw", align_bytes=64)
+        rows_dealt = sb.tile([P, 256], F32, name="rows_dealt", align_bytes=64)
+        cols = sb.tile([P, 256], F32, name="cols", align_bytes=64)
+        stat = [sb.tile([P, 1024], BF16, name="stat%d" % s, align_bytes=64) for s in range(2)]
+        q_bf = [sb.tile([P, 512], BF16, name="q_bf%d" % s, align_bytes=64) for s in range(2)]
+        v_bf = [sb.tile([P, 512], BF16, name="v_bf%d" % s, align_bytes=64) for s in range(2)]
+        o_bf = [sb.tile([P, 512], BF16, name="o_bf%d" % s, align_bytes=64) for s in range(2)]
+        sig = [sb.tile([P, PACK, W], F32, name="sig%d" % s) for s in range(2)]
+        res = [sb.tile([P, PACK * W], F32, name="res%d" % s) for s in range(2)]
+        c1 = sb.tile([P, 768], U32, name="c1", align_bytes=64)
+        s1 = sb.tile([P, 768], U8, name="s1", align_bytes=64)
+        c2 = sb.tile([P, 768], U32, name="c2", align_bytes=64)
+        s2 = sb.tile([P, 768], U8, name="s2", align_bytes=64)
+        oc = sb.tile([P, 256], U32, name="oc", align_bytes=64)
+        osc = sb.tile([P, 256], U8, name="osc", align_bytes=64)
+
+        def natural(x, s):
+            return x[4 * s : 4 * s + 4].rearrange("g (p j) c -> (g p) j c", j=PACK)
+
+        def live(s):
+            return stat[s][:].rearrange("p (x h c j) -> p x h c j", x=4, h=2, j=4)[:, :, s]
+
+        nc.vector.memset(rows_raw[:], 0.0)
+        for s in range(2):
+            nc.sync.dma_start(out=k_raw[s][:], in_=natural(kT, s))
+        for s in range(2):
+            nc.sync.dma_start(out=q_raw[s][:], in_=natural(qT, s))
+        for b, x in enumerate((kb, t)):
+            for h in range(2):
+                nc.scalar.dma_start(
+                    out=rows_raw[64 * h + b : 64 * h + 64 : 32, :],
+                    in_=x.rearrange("(a h s) i o -> h a (s i o)", a=2, h=2)[h],
+                )
+        for quad in range(4):
+            w0 = 4 * (quad % 2) + 2 * (quad // 2)
+            nc.sync.dma_start(
+                out=v_raw[R * quad : R * (quad + 1)].rearrange("p s j c -> p s (j c)"),
+                in_=v[w0 : w0 + 2].rearrange("s (p j) c -> p s (j c)", j=PACK),
+            )
+        for s in range(2):
+            nc.sync.dma_start(out=g_raw[s][:], in_=natural(og, s).rearrange("p j c -> p (j c)"))
+        for s in range(2):
+            nc.vector.memset(stat[s][:].bitcast(I32), 0)
+
+        def cast_k(s):
+            nc.vector.tensor_copy(
+                out=live(s).rearrange("p x c j -> p c x j"),
+                in_=k_raw[s][:].rearrange("p j (c x) -> p c x j", x=4),
+            )
+
+        def cast_q(s):
+            nc.vector.tensor_copy(
+                out=q_bf[s][:].rearrange("p (u c j) -> p c u j", u=4, j=4),
+                in_=q_raw[s][:].rearrange("p j (c u) -> p c u j", u=4),
+            )
+
+        cast_k(0)
+        nc.vector.tensor_copy(
+            out=rows_dealt[:].rearrange("p (s x c) -> p s x c", s=2, x=4),
+            in_=rows_raw[:].rearrange("p (s c x) -> p s x c", s=2, x=4),
+        )
+        quantize(nc, c1, s1, STAT[0], 256, stat[0][:])
+        cast_k(1)
+        nc.vector.transpose(out=cols[:], in_=rows_dealt[:])
+        quantize(nc, c1, s1, STAT[1], 256, stat[1][:])
+        for s in range(2):
+            cast_q(s)
+            quantize(nc, c1, s1, MOV[s], 128, q_bf[s][:])
+
+        products(nc, banks, c1, s1, (0, 2, 1, 3))
+
+        def weigh(s, x):
+            col = 32 * (4 * s + x)
+            for h in range(2):
+                part = slice(64 * h, 64 * h + 64)
+                nc.scalar.activation(
+                    out=sig[s][part, x, :],
+                    in_=banks[s + 2 * h][x // 2][part, (x % 2) * W : (x % 2 + 1) * W],
+                    func=ACT.Sigmoid,
+                    bias=cols[part, col : col + 1],
+                )
+            nc.vector.tensor_scalar(
+                out=live(s)[:, :, :, x],
+                in0=sig[s][:, x, :].rearrange("p (u c) -> p u c", u=4),
+                scalar1=cols[:, col + 1 : col + 2],
+                scalar2=None,
+                op0=ALU.mult,
+            )
+
+        def cast_v(s):
+            nc.vector.tensor_copy(
+                out=v_bf[s][:].rearrange("p (c j) -> p c j", j=4),
+                in_=v_raw[:, s].rearrange("p j c -> p c j"),
+            )
+
+        for x in range(4):
+            weigh(0, x)
+        cast_v(0)
+        quantize(nc, c2, s2, STAT[0], 256, stat[0][:])
+        weigh(1, 0)
+        cast_v(1)
+        weigh(1, 1)
+        quantize(nc, c2, s2, MOV[0], 128, v_bf[0][:])
+        weigh(1, 2)
+        quantize(nc, c2, s2, MOV[1], 128, v_bf[1][:])
+        weigh(1, 3)
+        quantize(nc, c2, s2, STAT[1], 256, stat[1][:])
+        for s in range(2):
+            nc.scalar.activation(out=gate[s][:], in_=g_raw[s][:], func=ACT.Sigmoid)
+
+        products(nc, banks, c2, s2, (0, 2, 1, 3))
+
+        def apply_gate(s):
+            for pair in range(2):
+                for h in range(2):
+                    part = slice(64 * h, 64 * h + 64)
+                    span = slice(256 * pair, 256 * pair + 256)
+                    nc.vector.scalar_tensor_tensor(
+                        out=res[s][part, span],
+                        in0=banks[s + 2 * h][pair][part, 0:256],
+                        scalar=1.0 / 16.0,
+                        in1=gate[s][part, span],
+                        op0=ALU.mult,
+                        op1=ALU.mult,
+                    )
+            nc.sync.dma_start(out=out_0[512 * s : 512 * (s + 1)].rearrange("(p u) e -> p (u e)", u=PACK), in_=res[s][:])
+
+        apply_gate(0)
+        nc.scalar.copy(
+            out=o_bf[0][:].rearrange("p (e u) -> p e u", u=4),
+            in_=res[0][:].rearrange("p (u e) -> p e u", u=4),
+        )
+        apply_gate(1)
+        quantize(nc, oc, osc, 0, 128, o_bf[0][:])
+        nc.vector.tensor_copy(
+            out=o_bf[1][:].rearrange("p (e u) -> p e u", u=4),
+            in_=res[1][:].rearrange("p (u e) -> p e u", u=4),
+        )
+        quantize(nc, oc, osc, 128, 128, o_bf[1][:])
+        nc.sync.dma_start(
+            out=out_1.rearrange("r x e u -> x r (e u)").bitcast(I32),
+            in_=oc[:].bitcast(I32).rearrange("p (r e) -> p r e", r=2),
+        )
+        for quad in range(4):
+            queue = nc.scalar if quad % 2 else nc.sync
+            queue.dma_start(
+                out=out_2[:, 4 * quad : 4 * quad + 4, :].rearrange("r f e -> f r e").bitcast(I32),
+                in_=osc[R * quad : R * quad + 4, :].bitcast(I32).rearrange("p (r e) -> p r e", r=2),
+            )

@@ -16,38 +16,15 @@ W = 128
 R = 32
 PACK = 4
 FLOPS = 2 * 2 * 8 * 128 * 128 * 128
-
-MOV = [0, 640]
-STAT = [128, 384]
+TILE_ORDER = (0, 2, 1, 3)
 
 
-def quantize(nc, codes, scales, start, words, staged):
-    nc.vector.quantize_mx(
-        out=codes[:, start : start + words].bitcast(FP8X4),
-        scales=scales[:, start : start + words],
-        in_=staged,
-    )
+def quantize(nc, codes, scales, staged):
+    nc.vector.quantize_mx(out=codes.bitcast(FP8X4), scales=scales, in_=staged)
 
 
-def products(nc, banks, codes, scales, order):
-    for pair in range(2):
-        for i in range(2):
-            place = 2 * pair + i
-            for slot in range(2):
-                for r in order:
-                    rows = slice(R * r, R * (r + 1))
-                    half = r // 2
-                    c0 = STAT[slot] + 64 * place - 64 * half
-                    m0 = MOV[slot]
-                    nc.tensor.matmul_mx(
-                        out=banks[r][pair][:, i * W : (i + 1) * W],
-                        lhsT=codes[rows, c0 : c0 + W].bitcast(FP8X4),
-                        lhsT_scale=scales[rows, c0 : c0 + W],
-                        rhs=codes[rows, m0 : m0 + W].bitcast(FP8X4),
-                        rhs_scale=scales[rows, m0 : m0 + W],
-                        start=(slot == 0),
-                        stop=(slot == 1),
-                    )
+def interleaved(dst, src):
+    return dict(out=dst.rearrange("p (c j) -> p c j", j=PACK), in_=src.rearrange("p j c -> p c j"))
 
 
 def tile_rows_pl_win_sig_gate_kernel(tc, kT, qT, kb, t, v, og, out_0, out_1, out_2):
@@ -57,155 +34,148 @@ def tile_rows_pl_win_sig_gate_kernel(tc, kT, qT, kb, t, v, og, out_0, out_1, out
         ps = ctx.enter_context(tc.psum_pool(name="ps", bufs=1))
         ctx.enter_context(tc.manual_schedule())
 
+        def pair(name, shape, dtype):
+            return [sb.tile(shape, dtype, name="%s%d" % (name, s), align_bytes=64) for s in range(2)]
+
         banks = [[ps.tile([P, 512], F32, name="bank%d_%d" % (r, b)) for b in range(2)] for r in range(4)]
-        k_raw = [sb.tile([P, PACK, W], F32, name="k_raw%d" % s) for s in range(2)]
-        q_raw = [sb.tile([P, PACK, W], F32, name="q_raw%d" % s) for s in range(2)]
-        g_raw = [sb.tile([P, PACK * W], F32, name="g_raw%d" % s) for s in range(2)]
-        gate = [sb.tile([P, PACK * W], F32, name="gate%d" % s) for s in range(2)]
-        v_raw = sb.tile([P, 2, PACK, W], F32, name="v_raw")
+        k_raw = pair("k_raw", [P, PACK, W], F32)
+        q_raw = pair("q_raw", [P, PACK, W], F32)
+        v_raw = pair("v_raw", [P, PACK, W], F32)
+        g_raw = pair("g_raw", [P, 4, W], F32)
+        gate = pair("gate", [P, 4, W], F32)
         rows_raw = sb.tile([P, 256], F32, name="rows_raw", align_bytes=64)
-        rows_dealt = sb.tile([P, 256], F32, name="rows_dealt", align_bytes=64)
         cols = sb.tile([P, 256], F32, name="cols", align_bytes=64)
-        stat = [sb.tile([P, 1024], BF16, name="stat%d" % s, align_bytes=64) for s in range(2)]
-        q_bf = [sb.tile([P, 512], BF16, name="q_bf%d" % s, align_bytes=64) for s in range(2)]
-        v_bf = [sb.tile([P, 512], BF16, name="v_bf%d" % s, align_bytes=64) for s in range(2)]
-        o_bf = [sb.tile([P, 512], BF16, name="o_bf%d" % s, align_bytes=64) for s in range(2)]
-        sig = [sb.tile([P, PACK, W], F32, name="sig%d" % s) for s in range(2)]
-        res = [sb.tile([P, PACK * W], F32, name="res%d" % s) for s in range(2)]
-        c1 = sb.tile([P, 768], U32, name="c1", align_bytes=64)
-        s1 = sb.tile([P, 768], U8, name="s1", align_bytes=64)
-        c2 = sb.tile([P, 768], U32, name="c2", align_bytes=64)
-        s2 = sb.tile([P, 768], U8, name="s2", align_bytes=64)
-        oc = sb.tile([P, 256], U32, name="oc", align_bytes=64)
+        k_bf = pair("k_bf", [P, 512], BF16)
+        q_bf = pair("q_bf", [P, 512], BF16)
+        v_bf = sb.tile([P, 1024], BF16, name="v_bf", align_bytes=64)
+        p_bf = pair("p_bf", [P, 512], BF16)
+        o_bf = pair("o_bf", [P, 512], BF16)
+        sig = pair("sig", [P, 4, W], F32)
+        p_tok = pair("p_tok", [P, 4, W], BF16)
+        p_row = pair("p_row", [P, PACK, W], BF16)
+        res = pair("res", [P, 4, W], F32)
+        o_q = pair("o_q", [P, 4, W], BF16)
+        o_row = pair("o_row", [P, PACK, W], BF16)
+        kc = pair("kc", [P, W], U32)
+        ks = pair("ks", [P, W], U8)
+        qc = pair("qc", [P, W], U32)
+        qs = pair("qs", [P, W], U8)
+        pc = pair("pc", [P, W], U32)
+        psc = pair("psc", [P, W], U8)
+        vc = sb.tile([P, 256], U32, name="vc", align_bytes=64)
+        vs = sb.tile([P, 256], U8, name="vs", align_bytes=64)
+        oc = pair("oc", [P, W], U32)
         osc = sb.tile([P, 256], U8, name="osc", align_bytes=64)
 
         def natural(x, s):
             return x[4 * s : 4 * s + 4].rearrange("g (p j) c -> (g p) j c", j=PACK)
 
-        def live(s):
-            return stat[s][:].rearrange("p (x h c j) -> p x h c j", x=4, h=2, j=4)[:, :, s]
-
-        nc.vector.memset(rows_raw[:], 0.0)
-        for s in range(2):
-            nc.sync.dma_start(out=k_raw[s][:], in_=natural(kT, s))
-        for s in range(2):
-            nc.sync.dma_start(out=q_raw[s][:], in_=natural(qT, s))
+        nc.gpsimd.memset(rows_raw[:], 0.0)
+        nc.sync.dma_start(out=k_raw[0][:], in_=natural(kT, 0))
+        nc.sync.dma_start(out=q_raw[0][:], in_=natural(qT, 0))
         for b, x in enumerate((kb, t)):
-            for h in range(2):
-                nc.scalar.dma_start(
-                    out=rows_raw[64 * h + b : 64 * h + 64 : 32, :],
-                    in_=x.rearrange("(a h s) i o -> h a (s i o)", a=2, h=2)[h],
-                )
-        for quad in range(4):
-            w0 = 4 * (quad % 2) + 2 * (quad // 2)
             nc.sync.dma_start(
-                out=v_raw[R * quad : R * (quad + 1)].rearrange("p s j c -> p s (j c)"),
-                in_=v[w0 : w0 + 2].rearrange("s (p j) c -> p s (j c)", j=PACK),
+                out=rows_raw[b:P:R, :].rearrange("p (g a) -> p g a", a=R),
+                in_=x.rearrange("g (c a) o -> c g (a o)", a=R),
             )
+        nc.sync.dma_start(out=k_raw[1][:], in_=natural(kT, 1))
+        nc.sync.dma_start(out=q_raw[1][:], in_=natural(qT, 1))
         for s in range(2):
-            nc.sync.dma_start(out=g_raw[s][:], in_=natural(og, s).rearrange("p j c -> p (j c)"))
+            nc.sync.dma_start(out=v_raw[s][:], in_=natural(v, s))
         for s in range(2):
-            nc.vector.memset(stat[s][:].bitcast(I32), 0)
+            nc.sync.dma_start(out=g_raw[s][:], in_=og[4 * s : 4 * s + 4].rearrange("g q e -> q g e"))
 
-        def cast_k(s):
-            nc.vector.tensor_copy(
-                out=live(s).rearrange("p x c j -> p c x j"),
-                in_=k_raw[s][:].rearrange("p j (c x) -> p c x j", x=4),
-            )
-
-        def cast_q(s):
-            nc.vector.tensor_copy(
-                out=q_bf[s][:].rearrange("p (u c j) -> p c u j", u=4, j=4),
-                in_=q_raw[s][:].rearrange("p j (c u) -> p c u j", u=4),
-            )
-
-        cast_k(0)
-        nc.vector.tensor_copy(
-            out=rows_dealt[:].rearrange("p (s x c) -> p s x c", s=2, x=4),
-            in_=rows_raw[:].rearrange("p (s c x) -> p s x c", s=2, x=4),
-        )
-        quantize(nc, c1, s1, STAT[0], 256, stat[0][:])
-        cast_k(1)
-        nc.vector.transpose(out=cols[:], in_=rows_dealt[:])
-        quantize(nc, c1, s1, STAT[1], 256, stat[1][:])
-        for s in range(2):
-            cast_q(s)
-            quantize(nc, c1, s1, MOV[s], 128, q_bf[s][:])
-
-        products(nc, banks, c1, s1, (0, 2, 1, 3))
-
-        def weigh(s, x):
-            col = 32 * (4 * s + x)
-            for h in range(2):
-                part = slice(64 * h, 64 * h + 64)
-                nc.scalar.activation(
-                    out=sig[s][part, x, :],
-                    in_=banks[s + 2 * h][x // 2][part, (x % 2) * W : (x % 2 + 1) * W],
-                    func=ACT.Sigmoid,
-                    bias=cols[part, col : col + 1],
+        def product(s, stage, lc, ls, rc, rs):
+            for r in TILE_ORDER:
+                rows = slice(R * r, R * (r + 1))
+                nc.tensor.matmul_mx(
+                    out=banks[r][stage][:, s * W : (s + 1) * W],
+                    lhsT=lc[rows].bitcast(FP8X4),
+                    lhsT_scale=ls[rows],
+                    rhs=rc[rows].bitcast(FP8X4),
+                    rhs_scale=rs[rows],
+                    start=True,
+                    stop=True,
                 )
-            nc.vector.tensor_scalar(
-                out=live(s)[:, :, :, x],
-                in0=sig[s][:, x, :].rearrange("p (u c) -> p u c", u=4),
-                scalar1=cols[:, col + 1 : col + 2],
-                scalar2=None,
-                op0=ALU.mult,
-            )
+
+        def regroup(dst, src, r):
+            nc.sync.dma_start(out=dst[R * r : R * (r + 1)], in_=src[:, r, :])
+
+        def scores(s):
+            nc.vector.tensor_copy(**interleaved(k_bf[s][:], k_raw[s][:]))
+            quantize(nc, kc[s][:], ks[s][:], k_bf[s][:])
+            nc.vector.tensor_copy(**interleaved(q_bf[s][:], q_raw[s][:]))
+            quantize(nc, qc[s][:], qs[s][:], q_bf[s][:])
+            product(s, 0, kc[s][:], ks[s][:], qc[s][:], qs[s][:])
+
+        def weigh(s):
+            for r in TILE_ORDER:
+                col = R * (4 * s + r)
+                nc.scalar.activation(
+                    out=sig[s][:, r, :],
+                    in_=banks[r][0][:, s * W : (s + 1) * W],
+                    func=ACT.Sigmoid,
+                    bias=cols[:, col : col + 1],
+                )
+                nc.vector.tensor_scalar(
+                    out=p_tok[s][:, r, :],
+                    in0=sig[s][:, r, :],
+                    scalar1=cols[:, col + 1 : col + 2],
+                    scalar2=None,
+                    op0=ALU.mult,
+                )
+                regroup(p_row[s], p_tok[s], r)
 
         def cast_v(s):
-            nc.vector.tensor_copy(
-                out=v_bf[s][:].rearrange("p (c j) -> p c j", j=4),
-                in_=v_raw[:, s].rearrange("p j c -> p c j"),
-            )
+            nc.vector.tensor_copy(**interleaved(v_bf[:, 512 * s : 512 * (s + 1)], v_raw[s][:]))
 
-        for x in range(4):
-            weigh(0, x)
+        def values(s):
+            nc.vector.tensor_copy(**interleaved(p_bf[s][:], p_row[s][:]))
+            quantize(nc, pc[s][:], psc[s][:], p_bf[s][:])
+            span = slice(s * W, (s + 1) * W)
+            product(s, 1, pc[s][:], psc[s][:], vc[:, span], vs[:, span])
+
+        def apply_gate(s, dst, move):
+            for r in TILE_ORDER:
+                nc.vector.scalar_tensor_tensor(
+                    out=dst[s][:, r, :],
+                    in0=banks[r][1][:, s * W : (s + 1) * W],
+                    scalar=1.0 / 16.0,
+                    in1=gate[s][:, r, :],
+                    op0=ALU.mult,
+                    op1=ALU.mult,
+                )
+                if move:
+                    regroup(o_row[s], o_q[s], r)
+
+        def store(s):
+            nc.scalar.dma_start(out=out_0[512 * s : 512 * (s + 1)].rearrange("(g q) e -> q g e", g=4), in_=res[s][:])
+
+        def planes(s):
+            nc.vector.tensor_copy(**interleaved(o_bf[s][:], o_row[s][:]))
+            quantize(nc, oc[s][:], osc[:, s * W : (s + 1) * W], o_bf[s][:])
+            nc.sync.dma_start(out=out_1[s].rearrange("x e u -> x (e u)").bitcast(I32), in_=oc[s][:].bitcast(I32))
+
+        scores(0)
+        nc.vector.transpose(out=cols[:], in_=rows_raw[:])
+        scores(1)
+        weigh(0)
         cast_v(0)
-        quantize(nc, c2, s2, STAT[0], 256, stat[0][:])
-        weigh(1, 0)
+        weigh(1)
         cast_v(1)
-        weigh(1, 1)
-        quantize(nc, c2, s2, MOV[0], 128, v_bf[0][:])
-        weigh(1, 2)
-        quantize(nc, c2, s2, MOV[1], 128, v_bf[1][:])
-        weigh(1, 3)
-        quantize(nc, c2, s2, STAT[1], 256, stat[1][:])
         for s in range(2):
             nc.scalar.activation(out=gate[s][:], in_=g_raw[s][:], func=ACT.Sigmoid)
-
-        products(nc, banks, c2, s2, (0, 2, 1, 3))
-
-        def apply_gate(s):
-            for pair in range(2):
-                for h in range(2):
-                    part = slice(64 * h, 64 * h + 64)
-                    span = slice(256 * pair, 256 * pair + 256)
-                    nc.vector.scalar_tensor_tensor(
-                        out=res[s][part, span],
-                        in0=banks[s + 2 * h][pair][part, 0:256],
-                        scalar=1.0 / 16.0,
-                        in1=gate[s][part, span],
-                        op0=ALU.mult,
-                        op1=ALU.mult,
-                    )
-            nc.sync.dma_start(out=out_0[512 * s : 512 * (s + 1)].rearrange("(p u) e -> p (u e)", u=PACK), in_=res[s][:])
-
-        apply_gate(0)
-        nc.scalar.copy(
-            out=o_bf[0][:].rearrange("p (e u) -> p e u", u=4),
-            in_=res[0][:].rearrange("p (u e) -> p e u", u=4),
-        )
-        apply_gate(1)
-        quantize(nc, oc, osc, 0, 128, o_bf[0][:])
-        nc.vector.tensor_copy(
-            out=o_bf[1][:].rearrange("p (e u) -> p e u", u=4),
-            in_=res[1][:].rearrange("p (u e) -> p e u", u=4),
-        )
-        quantize(nc, oc, osc, 128, 128, o_bf[1][:])
-        nc.sync.dma_start(
-            out=out_1.rearrange("r x e u -> x r (e u)").bitcast(I32),
-            in_=oc[:].bitcast(I32).rearrange("p (r e) -> p r e", r=2),
-        )
+        quantize(nc, vc[:], vs[:], v_bf[:])
+        values(0)
+        values(1)
+        apply_gate(0, o_q, True)
+        apply_gate(1, o_q, True)
+        apply_gate(0, res, False)
+        store(0)
+        apply_gate(1, res, False)
+        store(1)
+        planes(0)
+        planes(1)
         for quad in range(4):
             queue = nc.scalar if quad % 2 else nc.sync
             queue.dma_start(

@@ -45,8 +45,7 @@ def tile_rows_pl_win_sig_gate_kernel(tc, kT, qT, kb, t, v, og, out_0, out_1, out
         gate = pair("gate", [P, 4, W], F32)
         rows_raw = sb.tile([P, 256], F32, name="rows_raw", align_bytes=64)
         cols = sb.tile([P, 256], F32, name="cols", align_bytes=64)
-        k_bf = pair("k_bf", [P, 512], BF16)
-        q_bf = pair("q_bf", [P, 512], BF16)
+        kq_bf = pair("kq_bf", [P, 1024], BF16)
         v_bf = sb.tile([P, 1024], BF16, name="v_bf", align_bytes=64)
         p_bf = pair("p_bf", [P, 512], BF16)
         o_bf = pair("o_bf", [P, 512], BF16)
@@ -56,10 +55,8 @@ def tile_rows_pl_win_sig_gate_kernel(tc, kT, qT, kb, t, v, og, out_0, out_1, out
         res = pair("res", [P, 4, W], F32)
         o_q = pair("o_q", [P, 4, W], BF16)
         o_row = pair("o_row", [P, PACK, W], BF16)
-        kc = pair("kc", [P, W], U32)
-        ks = pair("ks", [P, W], U8)
-        qc = pair("qc", [P, W], U32)
-        qs = pair("qs", [P, W], U8)
+        kqc = pair("kqc", [P, 2 * W], U32)
+        kqs = pair("kqs", [P, 2 * W], U8)
         pc = pair("pc", [P, W], U32)
         psc = pair("psc", [P, W], U8)
         vc = sb.tile([P, 256], U32, name="vc", align_bytes=64)
@@ -89,7 +86,7 @@ def tile_rows_pl_win_sig_gate_kernel(tc, kT, qT, kb, t, v, og, out_0, out_1, out
             for r in TILE_ORDER:
                 rows = slice(R * r, R * (r + 1))
                 nc.tensor.matmul_mx(
-                    out=banks[r][stage][:, s * W : (s + 1) * W],
+                    out=banks[r][s][:, stage * W : (stage + 1) * W],
                     lhsT=lc[rows].bitcast(FP8X4),
                     lhsT_scale=ls[rows],
                     rhs=rc[rows].bitcast(FP8X4),
@@ -98,25 +95,31 @@ def tile_rows_pl_win_sig_gate_kernel(tc, kT, qT, kb, t, v, og, out_0, out_1, out
                     stop=True,
                 )
 
-        def regroup(dst, src, r):
-            nc.sync.dma_start(out=dst[R * r : R * (r + 1)], in_=src[:, r, :])
+        def regroup(dst, src, r, queue=nc.sync):
+            queue.dma_start(out=dst[R * r : R * (r + 1)], in_=src[:, r, :])
+
+        def cast_k(s):
+            nc.vector.tensor_copy(**interleaved(kq_bf[s][:, 0:512], k_raw[s][:]))
+
+        def cast_q(s):
+            nc.vector.tensor_copy(**interleaved(kq_bf[s][:, 512:1024], q_raw[s][:]))
 
         def scores(s):
-            nc.vector.tensor_copy(**interleaved(k_bf[s][:], k_raw[s][:]))
-            quantize(nc, kc[s][:], ks[s][:], k_bf[s][:])
-            nc.vector.tensor_copy(**interleaved(q_bf[s][:], q_raw[s][:]))
-            quantize(nc, qc[s][:], qs[s][:], q_bf[s][:])
-            product(s, 0, kc[s][:], ks[s][:], qc[s][:], qs[s][:])
+            product(s, 0, kqc[s][:, 0:W], kqs[s][:, 0:W], kqc[s][:, W : 2 * W], kqs[s][:, W : 2 * W])
 
-        def weigh(s):
+        def sigmoids(s):
             for r in TILE_ORDER:
                 col = R * (4 * s + r)
                 nc.scalar.activation(
                     out=sig[s][:, r, :],
-                    in_=banks[r][0][:, s * W : (s + 1) * W],
+                    in_=banks[r][s][:, 0:W],
                     func=ACT.Sigmoid,
                     bias=cols[:, col : col + 1],
                 )
+
+        def weigh(s, tiles):
+            for r in tiles:
+                col = R * (4 * s + r)
                 nc.vector.tensor_scalar(
                     out=p_tok[s][:, r, :],
                     in0=sig[s][:, r, :],
@@ -129,50 +132,64 @@ def tile_rows_pl_win_sig_gate_kernel(tc, kT, qT, kb, t, v, og, out_0, out_1, out
         def cast_v(s):
             nc.vector.tensor_copy(**interleaved(v_bf[:, 512 * s : 512 * (s + 1)], v_raw[s][:]))
 
-        def values(s):
+        def pack_p(s):
             nc.vector.tensor_copy(**interleaved(p_bf[s][:], p_row[s][:]))
+
+        def values(s):
             quantize(nc, pc[s][:], psc[s][:], p_bf[s][:])
             span = slice(s * W, (s + 1) * W)
             product(s, 1, pc[s][:], psc[s][:], vc[:, span], vs[:, span])
 
-        def apply_gate(s, dst, move):
-            for r in TILE_ORDER:
+        def apply_gate(s, dst, move, tiles=TILE_ORDER):
+            for r in tiles:
                 nc.vector.scalar_tensor_tensor(
                     out=dst[s][:, r, :],
-                    in0=banks[r][1][:, s * W : (s + 1) * W],
+                    in0=banks[r][s][:, W : 2 * W],
                     scalar=1.0 / 16.0,
                     in1=gate[s][:, r, :],
                     op0=ALU.mult,
                     op1=ALU.mult,
                 )
-                if move:
-                    regroup(o_row[s], o_q[s], r)
+                if move is not None:
+                    regroup(o_row[s], o_q[s], r, move)
 
         def store(s):
-            nc.scalar.dma_start(out=out_0[512 * s : 512 * (s + 1)].rearrange("(g q) e -> q g e", g=4), in_=res[s][:])
+            nc.sync.dma_start(out=out_0[512 * s : 512 * (s + 1)].rearrange("(g q) e -> q g e", g=4), in_=res[s][:])
 
         def planes(s):
             nc.vector.tensor_copy(**interleaved(o_bf[s][:], o_row[s][:]))
             quantize(nc, oc[s][:], osc[:, s * W : (s + 1) * W], o_bf[s][:])
             nc.sync.dma_start(out=out_1[s].rearrange("x e u -> x (e u)").bitcast(I32), in_=oc[s][:].bitcast(I32))
 
-        scores(0)
+        cast_k(0)
+        cast_q(0)
         nc.vector.transpose(out=cols[:], in_=rows_raw[:])
+        quantize(nc, kqc[0][:], kqs[0][:], kq_bf[0][:])
+        scores(0)
+        sigmoids(0)
+        cast_k(1)
+        cast_q(1)
+        quantize(nc, kqc[1][:, 0:W], kqs[1][:, 0:W], kq_bf[1][:, 0:512])
+        quantize(nc, kqc[1][:, W : 2 * W], kqs[1][:, W : 2 * W], kq_bf[1][:, 512:1024])
         scores(1)
-        weigh(0)
+        sigmoids(1)
+        weigh(0, TILE_ORDER)
         cast_v(0)
-        weigh(1)
+        weigh(1, TILE_ORDER)
         cast_v(1)
         for s in range(2):
             nc.scalar.activation(out=gate[s][:], in_=g_raw[s][:], func=ACT.Sigmoid)
         quantize(nc, vc[:], vs[:], v_bf[:])
+        pack_p(0)
         values(0)
+        pack_p(1)
+        apply_gate(0, o_q, nc.sync, TILE_ORDER[:1])
         values(1)
-        apply_gate(0, o_q, True)
-        apply_gate(1, o_q, True)
-        apply_gate(0, res, False)
+        apply_gate(0, o_q, nc.sync, TILE_ORDER[1:])
+        apply_gate(1, o_q, nc.sync)
+        apply_gate(0, res, None)
         store(0)
-        apply_gate(1, res, False)
+        apply_gate(1, res, None)
         store(1)
         planes(0)
         planes(1)

from contextlib import ExitStack

import concourse.mybir as mybir

F32 = mybir.dt.float32
BF16 = mybir.dt.bfloat16
I32 = mybir.dt.int32
U32 = mybir.dt.uint32
U8 = mybir.dt.uint8
FP8X4 = mybir.dt.float8_e4m3fn_x4
ALU = mybir.AluOpType
ACT = mybir.ActivationFunctionType

P = 128
W = 128
R = 32
PACK = 4
FLOPS = 2 * 2 * 8 * 128 * 128 * 128
TILE_ORDER = (0, 2, 1, 3)


def quantize(nc, codes, scales, staged):
    nc.vector.quantize_mx(out=codes.bitcast(FP8X4), scales=scales, in_=staged)


def interleaved(dst, src):
    return dict(out=dst.rearrange("p (c j) -> p c j", j=PACK), in_=src.rearrange("p j c -> p c j"))


def tile_rows_pl_win_sig_gate_kernel(tc, kT, qT, kb, t, v, og, out_0, out_1, out_2):
    nc = tc.nc
    with ExitStack() as ctx:
        sb = ctx.enter_context(tc.tile_pool(name="sb", bufs=1))
        ps = ctx.enter_context(tc.psum_pool(name="ps", bufs=1))
        ctx.enter_context(tc.manual_schedule())

        def pair(name, shape, dtype):
            return [sb.tile(shape, dtype, name="%s%d" % (name, s), align_bytes=64) for s in range(2)]

        banks = [[ps.tile([P, 512], F32, name="bank%d_%d" % (r, b)) for b in range(2)] for r in range(4)]
        k_raw = pair("k_raw", [P, PACK, W], F32)
        q_raw = pair("q_raw", [P, PACK, W], F32)
        v_raw = pair("v_raw", [P, PACK, W], F32)
        g_raw = pair("g_raw", [P, 4, W], F32)
        gate = pair("gate", [P, 4, W], F32)
        rows_raw = sb.tile([P, 256], F32, name="rows_raw", align_bytes=64)
        cols = sb.tile([P, 256], F32, name="cols", align_bytes=64)
        kq_bf = pair("kq_bf", [P, 1024], BF16)
        v_bf = sb.tile([P, 1024], BF16, name="v_bf", align_bytes=64)
        p_bf = pair("p_bf", [P, 512], BF16)
        o_bf = pair("o_bf", [P, 512], BF16)
        sig = pair("sig", [P, 4, W], F32)
        p_tok = pair("p_tok", [P, 4, W], BF16)
        p_row = pair("p_row", [P, PACK, W], BF16)
        res = pair("res", [P, 4, W], F32)
        o_q = pair("o_q", [P, 4, W], BF16)
        o_row = pair("o_row", [P, PACK, W], BF16)
        kqc = pair("kqc", [P, 2 * W], U32)
        kqs = pair("kqs", [P, 2 * W], U8)
        pc = pair("pc", [P, W], U32)
        psc = pair("psc", [P, W], U8)
        vc = sb.tile([P, 256], U32, name="vc", align_bytes=64)
        vs = sb.tile([P, 256], U8, name="vs", align_bytes=64)
        oc = pair("oc", [P, W], U32)
        osc = sb.tile([P, 256], U8, name="osc", align_bytes=64)

        def natural(x, s):
            return x[4 * s : 4 * s + 4].rearrange("g (p j) c -> (g p) j c", j=PACK)

        nc.gpsimd.memset(rows_raw[:], 0.0)
        nc.sync.dma_start(out=k_raw[0][:], in_=natural(kT, 0))
        nc.sync.dma_start(out=q_raw[0][:], in_=natural(qT, 0))
        for b, x in enumerate((kb, t)):
            nc.sync.dma_start(
                out=rows_raw[b:P:R, :].rearrange("p (g a) -> p g a", a=R),
                in_=x.rearrange("g (c a) o -> c g (a o)", a=R),
            )
        nc.sync.dma_start(out=k_raw[1][:], in_=natural(kT, 1))
        nc.sync.dma_start(out=q_raw[1][:], in_=natural(qT, 1))
        for s in range(2):
            nc.sync.dma_start(out=v_raw[s][:], in_=natural(v, s))
        for s in range(2):
            nc.sync.dma_start(out=g_raw[s][:], in_=og[4 * s : 4 * s + 4].rearrange("g q e -> q g e"))

        def product(s, stage, lc, ls, rc, rs):
            for r in TILE_ORDER:
                rows = slice(R * r, R * (r + 1))
                nc.tensor.matmul_mx(
                    out=banks[r][s][:, stage * W : (stage + 1) * W],
                    lhsT=lc[rows].bitcast(FP8X4),
                    lhsT_scale=ls[rows],
                    rhs=rc[rows].bitcast(FP8X4),
                    rhs_scale=rs[rows],
                    start=True,
                    stop=True,
                )

        def regroup(dst, src, r, queue=nc.sync):
            queue.dma_start(out=dst[R * r : R * (r + 1)], in_=src[:, r, :])

        def cast_k(s):
            nc.vector.tensor_copy(**interleaved(kq_bf[s][:, 0:512], k_raw[s][:]))

        def cast_q(s):
            nc.vector.tensor_copy(**interleaved(kq_bf[s][:, 512:1024], q_raw[s][:]))

        def scores(s):
            product(s, 0, kqc[s][:, 0:W], kqs[s][:, 0:W], kqc[s][:, W : 2 * W], kqs[s][:, W : 2 * W])

        def sigmoids(s):
            for r in TILE_ORDER:
                col = R * (4 * s + r)
                nc.scalar.activation(
                    out=sig[s][:, r, :],
                    in_=banks[r][s][:, 0:W],
                    func=ACT.Sigmoid,
                    bias=cols[:, col : col + 1],
                )

        def weigh(s, tiles):
            for r in tiles:
                col = R * (4 * s + r)
                nc.vector.tensor_scalar(
                    out=p_tok[s][:, r, :],
                    in0=sig[s][:, r, :],
                    scalar1=cols[:, col + 1 : col + 2],
                    scalar2=None,
                    op0=ALU.mult,
                )
                regroup(p_row[s], p_tok[s], r)

        def cast_v(s):
            nc.vector.tensor_copy(**interleaved(v_bf[:, 512 * s : 512 * (s + 1)], v_raw[s][:]))

        def pack_p(s):
            nc.vector.tensor_copy(**interleaved(p_bf[s][:], p_row[s][:]))

        def values(s):
            quantize(nc, pc[s][:], psc[s][:], p_bf[s][:])
            span = slice(s * W, (s + 1) * W)
            product(s, 1, pc[s][:], psc[s][:], vc[:, span], vs[:, span])

        def apply_gate(s, dst, move, tiles=TILE_ORDER):
            for r in tiles:
                nc.vector.scalar_tensor_tensor(
                    out=dst[s][:, r, :],
                    in0=banks[r][s][:, W : 2 * W],
                    scalar=1.0 / 16.0,
                    in1=gate[s][:, r, :],
                    op0=ALU.mult,
                    op1=ALU.mult,
                )
                if move is not None:
                    regroup(o_row[s], o_q[s], r, move)

        def store(s):
            nc.sync.dma_start(out=out_0[512 * s : 512 * (s + 1)].rearrange("(g q) e -> q g e", g=4), in_=res[s][:])

        def planes(s):
            nc.vector.tensor_copy(**interleaved(o_bf[s][:], o_row[s][:]))
            quantize(nc, oc[s][:], osc[:, s * W : (s + 1) * W], o_bf[s][:])
            nc.sync.dma_start(out=out_1[s].rearrange("x e u -> x (e u)").bitcast(I32), in_=oc[s][:].bitcast(I32))

        cast_k(0)
        cast_q(0)
        nc.vector.transpose(out=cols[:], in_=rows_raw[:])
        quantize(nc, kqc[0][:], kqs[0][:], kq_bf[0][:])
        scores(0)
        sigmoids(0)
        cast_k(1)
        cast_q(1)
        quantize(nc, kqc[1][:, 0:W], kqs[1][:, 0:W], kq_bf[1][:, 0:512])
        quantize(nc, kqc[1][:, W : 2 * W], kqs[1][:, W : 2 * W], kq_bf[1][:, 512:1024])
        scores(1)
        sigmoids(1)
        weigh(0, TILE_ORDER)
        cast_v(0)
        weigh(1, TILE_ORDER)
        cast_v(1)
        for s in range(2):
            nc.scalar.activation(out=gate[s][:], in_=g_raw[s][:], func=ACT.Sigmoid)
        quantize(nc, vc[:], vs[:], v_bf[:])
        pack_p(0)
        values(0)
        pack_p(1)
        apply_gate(0, o_q, nc.sync, TILE_ORDER[:1])
        values(1)
        apply_gate(0, o_q, nc.sync, TILE_ORDER[1:])
        apply_gate(1, o_q, nc.sync)
        apply_gate(0, res, None)
        store(0)
        apply_gate(1, res, None)
        store(1)
        planes(0)
        planes(1)
        for quad in range(4):
            queue = nc.scalar if quad % 2 else nc.sync
            queue.dma_start(
                out=out_2[:, 4 * quad : 4 * quad + 4, :].rearrange("r f e -> f r e").bitcast(I32),
                in_=osc[R * quad : R * quad + 4, :].bitcast(I32).rearrange("p (r e) -> p r e", r=2),
            )
